import numpy as np
import ml_dtypes


def mxq(x, axis, fmt="e4m3"):
    dtype, down = {"e4m3": (ml_dtypes.float8_e4m3fn, 7), "e5m2": (ml_dtypes.float8_e5m2, 14)}[fmt]
    v = np.moveaxis(np.asarray(x, np.float32).astype(ml_dtypes.bfloat16).astype(np.float64), axis, -1)
    blocks = v.reshape(v.shape[:-1] + (-1, 32))
    amax = np.abs(blocks).max(-1, keepdims=True)
    byte = np.maximum(np.where(amax > 0, np.frexp(amax)[1] - 1 + 127, 0) - down, 1)
    scale = np.exp2(byte - 127.0)
    codes = (blocks / scale).astype(np.float32).astype(dtype).astype(np.float64)
    return np.moveaxis((codes * scale).reshape(v.shape), -1, axis)


WIDE = False


def mx_kscale(k):
    if not WIDE:
        return np.ones(k)
    levels = np.array([10, -10, 5, -5, 0])
    if k % 512:
        return np.exp2(np.random.permutation(np.resize(levels, k // 32))).repeat(32)
    a = np.empty((k // 512, 16))
    for p in range(k // 512):
        a[p, :8] = np.random.permutation(np.resize(levels, 8))
        for g in range(8):
            far = levels[np.abs(levels - a[p, g]) >= 10]
            a[p, g + 8] = far[np.random.randint(len(far))]
    return np.exp2(a.ravel()).repeat(32)


BF16 = ml_dtypes.bfloat16


def bf(x):
    return np.asarray(x, np.float32).astype(BF16)


def f64(x):
    return np.asarray(x).astype(np.float64)


E2M1 = np.array([0.0, 0.5, 1.0, 1.5, 2.0, 3.0, 4.0, 6.0, -0.0, -0.5, -1.0, -1.5, -2.0, -3.0, -4.0, -6.0])


def pack_weight(w, fmt):
    k, n = w.shape
    w = f64(bf(w)).reshape(k // 32, 32, n)
    amax = np.abs(w).max(1)
    if fmt == "e4m3":
        byte = np.frexp(amax)[1] - 1 + 127 - 7
    else:
        mant, ex = np.frexp(amax / 6.0)
        byte = np.where(mant > 0.5, ex, ex - 1) + 127
    byte = np.clip(np.where(amax > 0, byte, 1), 1, 254)
    scaled = (w * np.exp2(127.0 - byte)[:, None, :]).reshape(k, n).astype(np.float32)
    by_word = np.ascontiguousarray(scaled.reshape(k // 512, 128, 4, n).transpose(0, 1, 3, 2))
    if fmt == "e4m3":
        words = by_word.astype(ml_dtypes.float8_e4m3fn).view(np.uint8)
    else:
        c = by_word.astype(ml_dtypes.float4_e2m1fn).view(np.uint8) & 0xF
        words = c[..., 0::2] | (c[..., 1::2] << 4)
    return np.ascontiguousarray(words), np.ascontiguousarray(byte.astype(np.uint8).reshape(k // 512, 16, n))


def unpack_weight(words, scales, fmt):
    g, p, n, _ = words.shape
    if fmt == "e4m3":
        vals = np.ascontiguousarray(words).view(ml_dtypes.float8_e4m3fn).astype(np.float64)
    else:
        nib = np.empty((g, p, n, 4), np.uint8)
        nib[..., 0::2] = words & 0xF
        nib[..., 1::2] = words >> 4
        vals = E2M1[nib]
    vals = vals * np.repeat(np.exp2(scales.astype(np.float64) - 127.0), 8, axis=1)[..., None]
    return vals.transpose(0, 1, 3, 2).reshape(g * 512, n)
def pack4(w):
    words, scales = pack_weight(w, "e2m1")
    return words.reshape(words.shape[0], 128, -1), scales


def unpack4(words, scales):
    return unpack_weight(words.reshape(words.shape[0], 128, -1, 2), scales, "e2m1")


M, C, T, N = 1024, 512, 1024, 1024


def setup_inputs():
    s = mx_kscale(2 * C)
    t = mx_kscale(2 * T)
    load = np.exp(0.3 * np.random.standard_normal((C, 1)))
    qam = 2.0 * np.random.randint(0, 4, (2 * C, M)) - 3.0
    sym = qam * np.concatenate([load, load], axis=0)
    phase = np.random.uniform(0.0, 2.0 * np.pi, (C, 1))
    theta = 2.0 * np.pi * np.arange(C)[:, None] * np.arange(T)[None, :] / T + phase
    co, si = np.cos(theta), np.sin(theta)
    basis = np.block([[co, si], [-si, co]]) * np.sqrt(0.2 / C)
    sym_words, sym_scales = pack4(sym * s[:, None])
    idft_words, idft_scales = pack4(basis / s[:, None])
    fir = np.random.standard_normal((2 * T, N)) / np.sqrt(2 * T)
    fir_words, fir_scales = pack_weight(fir / t[:, None], "e4m3")
    return {"sym_words": sym_words, "sym_scales": sym_scales,
            "idft_words": idft_words, "idft_scales": idft_scales,
            "window": bf((1.0 + 0.2 * np.random.standard_normal(2 * T)) * t),
            "fir_words": fir_words, "fir_scales": fir_scales,
            "leak": bf(0.3 * np.random.standard_normal(N))}


def reference(sym_words, sym_scales, idft_words, idft_scales, window, fir_words, fir_scales, leak):
    x = unpack4(sym_words, sym_scales)
    b = unpack4(idft_words, idft_scales)
    y = x.T @ b
    z = np.tanh(y) * f64(window)
    h = unpack_weight(fir_words, fir_scales, "e4m3")
    return (mxq(z, 1, "e4m3") @ h) + f64(leak)

@@ -1,0 +1,190 @@
+from contextlib import ExitStack
+
+import concourse.mybir as mybir
+
+SYMBOLS, CARRIERS, SAMPLES, OUTPUTS = 1024, 1024, 2048, 1024
+FLOPS = 2 * SYMBOLS * CARRIERS * SAMPLES + 2 * SYMBOLS * SAMPLES * OUTPUTS
+
+F32 = mybir.dt.float32
+BF16 = mybir.dt.bfloat16
+I32 = mybir.dt.int32
+U32 = mybir.dt.uint32
+U8 = mybir.dt.uint8
+FP4X4 = mybir.dt.float4_e2m1fn_x4
+FP8X4 = mybir.dt.float8_e4m3fn_x4
+ACT = mybir.ActivationFunctionType
+ALU = mybir.AluOpType
+
+P = 128
+PACK = 4
+K_PASS = P * PACK
+PASSES_1 = CARRIERS // K_PASS
+PASSES_2 = SAMPLES // K_PASS
+QUARTER = 256
+QUARTERS = SYMBOLS // QUARTER
+BANK = 512
+SCALAR_UNITS = 5
+
+
+def tile_ofdm_clipped_transmit_s4_kernel(
+    tc, sym_words, sym_scales, idft_words, idft_scales, window, fir_words, fir_scales, leak, out
+):
+    nc = tc.nc
+    with ExitStack() as ctx:
+        keep = ctx.enter_context(tc.tile_pool(name="keep", bufs=1))
+        work = ctx.enter_context(tc.tile_pool(name="work", bufs=4))
+        psum = ctx.enter_context(tc.psum_pool(name="psum", bufs=8))
+        ctx.enter_context(tc.manual_schedule())
+
+        b_raw = [keep.tile([P, PASSES_1, 2 * K_PASS], U8, name="b_raw%d" % g, align_bytes=64) for g in range(PASSES_2)]
+        b_raw_scale = [keep.tile([P, PASSES_1, SAMPLES // 2], U8, name="b_raw_scale%d" % h, align_bytes=64) for h in range(2)]
+        x_words = [keep.tile([P, PASSES_1, SYMBOLS], U8, name="x_words%d" % h, align_bytes=64) for h in range(2)]
+        x_scale = [keep.tile([P, PASSES_1, SYMBOLS // 2], U8, name="x_scale%d" % h, align_bytes=64) for h in range(2)]
+        h_words = [keep.tile([P, OUTPUTS], U32, name="h_words%d" % g, align_bytes=64) for g in range(PASSES_2)]
+        h_scale = keep.tile([P, OUTPUTS], U8, align_bytes=64)
+        window_bf = keep.tile([P, PASSES_2, PACK], BF16)
+        window_f32 = keep.tile([P, PASSES_2, 1, PACK], F32)
+        leak_rows = keep.tile([P, OUTPUTS], BF16)
+
+        def flat(t):
+            return t[:].rearrange("p g n -> p (g n)").bitcast(I32)
+
+        for h in range(2):
+            nc.vector.memset(flat(b_raw_scale[h]), 0)
+            nc.vector.memset(flat(x_scale[h]), 0)
+        nc.vector.memset(h_scale[:].bitcast(I32), 0)
+
+        def load_b(g):
+            cols = slice(g * 2 * K_PASS, (g + 1) * 2 * K_PASS)
+            nc.sync.dma_start(out=b_raw[g][:].bitcast(I32), in_=idft_words[:, :, cols].rearrange("g p n -> p g n").bitcast(I32))
+
+        def load_x(h, queue):
+            cols = slice(h * SYMBOLS, (h + 1) * SYMBOLS)
+            queue.dma_start(out=x_words[h][:].bitcast(I32), in_=sym_words[:, :, cols].rearrange("g p n -> p g n").bitcast(I32))
+
+        def load_scale_rows(planes, scales, h, q, queue):
+            width = planes[h].shape[2]
+            queue.dma_start(
+                out=planes[h][32 * q : 32 * q + 4, :, :].bitcast(I32),
+                in_=scales[:, 4 * q : 4 * q + 4, h * width : (h + 1) * width].rearrange("g r n -> r g n").bitcast(I32),
+            )
+
+        load_b(0)
+        load_x(0, nc.scalar)
+        for q in range(4):
+            load_scale_rows(b_raw_scale, idft_scales, 0, q, nc.sync)
+        for q in range(4):
+            load_scale_rows(x_scale, sym_scales, 0, q, nc.scalar if q < 2 else nc.sync)
+        load_b(1)
+        load_b(2)
+        for q in range(4):
+            load_scale_rows(b_raw_scale, idft_scales, 1, q, nc.sync)
+        load_b(3)
+        nc.sync.dma_start(out=window_bf[:], in_=window.rearrange("(g p t) -> p g t", g=PASSES_2, t=PACK))
+        load_x(1, nc.sync)
+        for q in range(4):
+            load_scale_rows(x_scale, sym_scales, 1, q, nc.sync)
+        for q in range(4):
+            nc.sync.dma_start(out=h_scale[32 * q : 32 * q + 16, :].bitcast(I32), in_=fir_scales[:, 4 * q : 4 * q + 4, :].bitcast(I32))
+        for g in range(PASSES_2):
+            nc.sync.dma_start(out=h_words[g][:].bitcast(I32), in_=fir_words[g].rearrange("p n t -> p (n t)").bitcast(I32))
+        nc.sync.dma_start(out=leak_rows[:], in_=leak.partition_broadcast(P))
+
+        b_words, b_scale = {}, {}
+        for g in range(PASSES_2):
+            for u in range(2):
+                words = keep.tile([P, PASSES_1, 2, P, 2], U8, name="b_words%d%d" % (g, u), align_bytes=64)
+                scale = keep.tile([P, PASSES_1, 2, P], U8, name="b_scale%d%d" % (g, u), align_bytes=64)
+                src = b_raw[g][:].rearrange("p c (m t b) -> p c t m b", t=PACK, b=2)
+                nc.vector.tensor_copy(out=words[:], in_=src[:, :, 2 * u : 2 * u + 2, :, :])
+                src = b_raw_scale[g // 2][:, :, g % 2 * K_PASS : (g % 2 + 1) * K_PASS].rearrange("p c (m t) -> p c t m", t=PACK)
+                nc.vector.tensor_copy(out=scale[:], in_=src[:, :, 2 * u : 2 * u + 2, :])
+                b_words[g, u], b_scale[g, u] = words, scale
+        nc.vector.tensor_copy(out=window_f32[:].rearrange("p g o t -> p g (o t)"), in_=window_bf[:])
+
+        units = [(q, g) for q in range(QUARTERS) for g in range(PASSES_2)]
+        vector_units, scalar_units = units[:-SCALAR_UNITS], units[-SCALAR_UNITS:]
+        first_sweep = [(q, g) for g in range(PASSES_2) for q in range(2)]
+        clipped = {}
+        for q, g in first_sweep + units[len(first_sweep) :]:
+            clip = keep.tile([P, 2, BANK], F32, name="clip%d%d" % (q, g))
+            clipped[q, g] = clip
+            word_cols = slice((q % 2) * 2 * QUARTER, (q % 2 + 1) * 2 * QUARTER)
+            for u in range(2):
+                bank = psum.tile([P, BANK], F32, name="bank")
+                for e in range(2):
+                    for c in range(PASSES_1):
+                        nc.tensor.matmul_mx(
+                            out=bank[:, e * QUARTER : (e + 1) * QUARTER],
+                            lhsT=b_words[g, u][:, c, e, :, :].rearrange("p m b -> p (m b)").bitcast(FP4X4),
+                            lhsT_scale=b_scale[g, u][:, c, e, :],
+                            rhs=x_words[q // 2][:, c, word_cols].bitcast(FP4X4),
+                            rhs_scale=x_scale[q // 2][:, c, q % 2 * QUARTER : (q % 2 + 1) * QUARTER],
+                            start=(c == 0),
+                            stop=(c == PASSES_1 - 1),
+                        )
+                if (q, g) in vector_units:
+                    nc.scalar.activation(
+                        out=clip[:, u, :].rearrange("p (m e) -> p m e", e=2),
+                        in_=bank[:].rearrange("p (e m) -> p m e", e=2),
+                        func=ACT.Tanh,
+                    )
+                else:
+                    nc.scalar.activation(out=clip[:, u, :], in_=bank[:], func=ACT.Tanh)
+
+        shaped, z_words, z_scale = {}, {}, {}
+
+        def shape_on_vector(q, g):
+            z = work.tile([P, QUARTER * PACK], BF16, name="z_vector", align_bytes=64)
+            shaped[q, g] = z
+            nc.vector.tensor_tensor(
+                out=z[:].rearrange("p (m u e) -> p m u e", u=2, e=2),
+                in0=clipped[q, g][:].rearrange("p u (m e) -> p m u e", e=2),
+                in1=window_f32[:, g, :, :].rearrange("p o (u e) -> p o u e", e=2).to_broadcast([P, QUARTER, 2, 2]),
+                op=ALU.mult,
+            )
+
+        def shape_on_scalar(q, g):
+            rows = work.tile([P, PACK, QUARTER], BF16, name="z_rows", bufs=2)
+            z = keep.tile([P, QUARTER * PACK], BF16, name="z_scalar%d%d" % (q, g), align_bytes=64)
+            shaped[q, g] = z
+            src = clipped[q, g][:].rearrange("p u (e m) -> p (u e) m", e=2)
+            for t in range(PACK):
+                nc.scalar.activation(out=rows[:, t, :], in_=src[:, t, :], func=ACT.Copy, scale=window_f32[:, g, 0, t : t + 1])
+            nc.scalar.copy(out=z[:].rearrange("p (m t) -> p m t", t=PACK), in_=rows[:].rearrange("p t m -> p m t"))
+
+        def quantise(q, g):
+            words = keep.tile([P, QUARTER], U32, name="z_words%d%d" % (q, g), align_bytes=64)
+            scale = keep.tile([P, QUARTER], U8, name="z_scale%d%d" % (q, g), align_bytes=64)
+            nc.vector.quantize_mx(out=words[:].bitcast(FP8X4), scales=scale[:], in_=shaped[q, g][:])
+            z_words[q, g], z_scale[q, g] = words, scale
+
+        for i, unit in enumerate(vector_units):
+            shape_on_vector(*unit)
+            if i > 0:
+                quantise(*vector_units[i - 1])
+        for unit in scalar_units:
+            shape_on_scalar(*unit)
+
+        to_quantise = vector_units[-1:] + scalar_units
+        groups = [(m0, n0, BANK) for m0 in range(0, SYMBOLS, P) for n0 in range(0, OUTPUTS, BANK)]
+        last_m0, last_n0, width = groups.pop()
+        groups.extend([(last_m0, last_n0, width // 2), (last_m0, last_n0 + width // 2, width // 2)])
+        for j, (m0, n0, width) in enumerate(groups):
+            q, m_cols, n_cols = m0 // QUARTER, slice(m0 % QUARTER, m0 % QUARTER + P), slice(n0, n0 + width)
+            bank = psum.tile([P, BANK], F32, name="bank")
+            for g in range(PASSES_2):
+                nc.tensor.matmul_mx(
+                    out=bank[:, :width],
+                    lhsT=z_words[q, g][:, m_cols].bitcast(FP8X4),
+                    lhsT_scale=z_scale[q, g][:, m_cols],
+                    rhs=h_words[g][:, n_cols].bitcast(FP8X4),
+                    rhs_scale=h_scale[4 * g :, n_cols],
+                    start=(g == 0),
+                    stop=(g == PASSES_2 - 1),
+                )
+            result = work.tile([P, BANK], F32, name="result", bufs=8)
+            nc.vector.tensor_tensor(out=result[:, :width], in0=bank[:, :width], in1=leak_rows[:, n_cols], op=ALU.add)
+            nc.sync.dma_start(out=out[m0 : m0 + P, n_cols], in_=result[:, :width])
+            if j % 2 == 0 and j // 2 < len(to_quantise):
+                quantise(*to_quantise[j // 2])

@@ -23,7 +23,7 @@ PASSES_2 = SAMPLES // K_PASS
 QUARTER = 256
 QUARTERS = SYMBOLS // QUARTER
 BANK = 512
-SCALAR_UNITS = 5
+SCALAR_UNITS = 4
 
 
 def tile_ofdm_clipped_transmit_s4_kernel(
@@ -132,7 +132,7 @@ def tile_ofdm_clipped_transmit_s4_kernel(
                 else:
                     nc.scalar.activation(out=clip[:, u, :], in_=bank[:], func=ACT.Tanh)
 
-        shaped, z_words, z_scale = {}, {}, {}
+        z_rows, shaped, z_words, z_scale = {}, {}, {}, {}
 
         def shape_on_vector(q, g):
             z = work.tile([P, QUARTER * PACK], BF16, name="z_vector", align_bytes=64)
@@ -144,14 +144,17 @@ def tile_ofdm_clipped_transmit_s4_kernel(
                 op=ALU.mult,
             )
 
-        def shape_on_scalar(q, g):
-            rows = work.tile([P, PACK, QUARTER], BF16, name="z_rows", bufs=2)
-            z = keep.tile([P, QUARTER * PACK], BF16, name="z_scalar%d%d" % (q, g), align_bytes=64)
-            shaped[q, g] = z
+        def scale_on_scalar(q, g):
+            rows = work.tile([P, PACK, QUARTER], BF16, name="z_rows")
+            z_rows[q, g] = rows
             src = clipped[q, g][:].rearrange("p u (e m) -> p (u e) m", e=2)
             for t in range(PACK):
                 nc.scalar.activation(out=rows[:, t, :], in_=src[:, t, :], func=ACT.Copy, scale=window_f32[:, g, 0, t : t + 1])
-            nc.scalar.copy(out=z[:].rearrange("p (m t) -> p m t", t=PACK), in_=rows[:].rearrange("p t m -> p m t"))
+
+        def interleave_on_scalar(q, g):
+            z = keep.tile([P, QUARTER * PACK], BF16, name="z_scalar%d%d" % (q, g), align_bytes=64)
+            shaped[q, g] = z
+            nc.scalar.copy(out=z[:].rearrange("p (m t) -> p m t", t=PACK), in_=z_rows[q, g][:].rearrange("p t m -> p m t"))
 
         def quantise(q, g):
             words = keep.tile([P, QUARTER], U32, name="z_words%d%d" % (q, g), align_bytes=64)
@@ -163,8 +166,11 @@ def tile_ofdm_clipped_transmit_s4_kernel(
             shape_on_vector(*unit)
             if i > 0:
                 quantise(*vector_units[i - 1])
-        for unit in scalar_units:
-            shape_on_scalar(*unit)
+        for i, unit in enumerate(scalar_units):
+            scale_on_scalar(*unit)
+            if i > 0:
+                interleave_on_scalar(*scalar_units[i - 1])
+        interleave_on_scalar(*scalar_units[-1])
 
         to_quantise = vector_units[-1:] + scalar_units
         groups = [(m0, n0, BANK) for m0 in range(0, SYMBOLS, P) for n0 in range(0, OUTPUTS, BANK)]

@@ -24,6 +24,8 @@ QUARTER = 256
 QUARTERS = SYMBOLS // QUARTER
 BANK = 512
 SCALAR_UNITS = 4
+RUN = 4
+WARM_PASSES = 3
 
 
 def tile_ofdm_clipped_transmit_s4_kernel(
@@ -43,7 +45,7 @@ def tile_ofdm_clipped_transmit_s4_kernel(
         h_words = [keep.tile([P, OUTPUTS], U32, name="h_words%d" % g, align_bytes=64) for g in range(PASSES_2)]
         h_scale = keep.tile([P, OUTPUTS], U8, align_bytes=64)
         window_bf = keep.tile([P, PASSES_2, PACK], BF16)
-        window_f32 = keep.tile([P, PASSES_2, 1, PACK], F32)
+        window_f32 = keep.tile([P, PASSES_2, 1, PACK, 1], F32)
         leak_rows = keep.tile([P, OUTPUTS], BF16)
 
         def flat(t):
@@ -100,37 +102,44 @@ def tile_ofdm_clipped_transmit_s4_kernel(
                 src = b_raw_scale[g // 2][:, :, g % 2 * K_PASS : (g % 2 + 1) * K_PASS].rearrange("p c (m t) -> p c t m", t=PACK)
                 nc.vector.tensor_copy(out=scale[:], in_=src[:, :, 2 * u : 2 * u + 2, :])
                 b_words[g, u], b_scale[g, u] = words, scale
-        nc.vector.tensor_copy(out=window_f32[:].rearrange("p g o t -> p g (o t)"), in_=window_bf[:])
+        nc.vector.tensor_copy(out=window_f32[:].rearrange("p g o t i -> p g (o t i)"), in_=window_bf[:])
 
         units = [(q, g) for q in range(QUARTERS) for g in range(PASSES_2)]
-        vector_units, scalar_units = units[:-SCALAR_UNITS], units[-SCALAR_UNITS:]
-        first_sweep = [(q, g) for g in range(PASSES_2) for q in range(2)]
+        first_half = [(q, g) for g in range(PASSES_2) for q in range(2)]
+        vector_units, scalar_units = first_half + units[len(first_half) : -SCALAR_UNITS], units[-SCALAR_UNITS:]
+        for i in range(WARM_PASSES):
+            bank = psum.tile([P, BANK], F32, name="bank")
+            nc.tensor.matmul_mx(
+                out=bank[:],
+                lhsT=b_raw[0][:, 0, : 2 * P].bitcast(FP4X4),
+                lhsT_scale=b_raw_scale[0][:, 0, :P],
+                rhs=b_raw[0][:, 0, :].bitcast(FP4X4),
+                rhs_scale=b_raw_scale[0][:, 0, :BANK],
+                start=True,
+                stop=True,
+            )
+
         clipped = {}
-        for q, g in first_sweep + units[len(first_sweep) :]:
-            clip = keep.tile([P, 2, BANK], F32, name="clip%d%d" % (q, g))
-            clipped[q, g] = clip
-            word_cols = slice((q % 2) * 2 * QUARTER, (q % 2 + 1) * 2 * QUARTER)
-            for u in range(2):
-                bank = psum.tile([P, BANK], F32, name="bank")
-                for e in range(2):
+        for h in range(2):
+            for g in range(PASSES_2):
+                clip = keep.tile([P, PACK, BANK], F32, name="clip%d%d" % (h, g))
+                clipped[h, g] = clip
+                for t in range(PACK):
+                    bank = psum.tile([P, BANK], F32, name="bank")
                     for c in range(PASSES_1):
                         nc.tensor.matmul_mx(
-                            out=bank[:, e * QUARTER : (e + 1) * QUARTER],
-                            lhsT=b_words[g, u][:, c, e, :, :].rearrange("p m b -> p (m b)").bitcast(FP4X4),
-                            lhsT_scale=b_scale[g, u][:, c, e, :],
-                            rhs=x_words[q // 2][:, c, word_cols].bitcast(FP4X4),
-                            rhs_scale=x_scale[q // 2][:, c, q % 2 * QUARTER : (q % 2 + 1) * QUARTER],
+                            out=bank[:],
+                            lhsT=b_words[g, t // 2][:, c, t % 2, :, :].rearrange("p m b -> p (m b)").bitcast(FP4X4),
+                            lhsT_scale=b_scale[g, t // 2][:, c, t % 2, :],
+                            rhs=x_words[h][:, c, :].bitcast(FP4X4),
+                            rhs_scale=x_scale[h][:, c, :],
                             start=(c == 0),
                             stop=(c == PASSES_1 - 1),
                         )
-                if (q, g) in vector_units:
-                    nc.scalar.activation(
-                        out=clip[:, u, :].rearrange("p (m e) -> p m e", e=2),
-                        in_=bank[:].rearrange("p (e m) -> p m e", e=2),
-                        func=ACT.Tanh,
-                    )
-                else:
-                    nc.scalar.activation(out=clip[:, u, :], in_=bank[:], func=ACT.Tanh)
+                    nc.scalar.activation(out=clip[:, t, :], in_=bank[:], func=ACT.Tanh)
+
+        def clip_of(q, g):
+            return clipped[q // 2, g][:, :, q % 2 * QUARTER : (q % 2 + 1) * QUARTER]
 
         z_rows, shaped, z_words, z_scale = {}, {}, {}, {}
 
@@ -138,23 +147,26 @@ def tile_ofdm_clipped_transmit_s4_kernel(
             z = work.tile([P, QUARTER * PACK], BF16, name="z_vector", align_bytes=64)
             shaped[q, g] = z
             nc.vector.tensor_tensor(
-                out=z[:].rearrange("p (m u e) -> p m u e", u=2, e=2),
-                in0=clipped[q, g][:].rearrange("p u (m e) -> p m u e", e=2),
-                in1=window_f32[:, g, :, :].rearrange("p o (u e) -> p o u e", e=2).to_broadcast([P, QUARTER, 2, 2]),
+                out=z[:].rearrange("p (c i t) -> p c t i", i=RUN, t=PACK),
+                in0=clip_of(q, g).rearrange("p t (c i) -> p c t i", i=RUN),
+                in1=window_f32[:, g, :, :, :].to_broadcast([P, QUARTER // RUN, PACK, RUN]),
                 op=ALU.mult,
             )
 
         def scale_on_scalar(q, g):
             rows = work.tile([P, PACK, QUARTER], BF16, name="z_rows")
             z_rows[q, g] = rows
-            src = clipped[q, g][:].rearrange("p u (e m) -> p (u e) m", e=2)
+            src = clip_of(q, g)
             for t in range(PACK):
-                nc.scalar.activation(out=rows[:, t, :], in_=src[:, t, :], func=ACT.Copy, scale=window_f32[:, g, 0, t : t + 1])
+                nc.scalar.activation(out=rows[:, t, :], in_=src[:, t, :], func=ACT.Copy, scale=window_f32[:, g, 0, t, :])
 
         def interleave_on_scalar(q, g):
             z = keep.tile([P, QUARTER * PACK], BF16, name="z_scalar%d%d" % (q, g), align_bytes=64)
             shaped[q, g] = z
-            nc.scalar.copy(out=z[:].rearrange("p (m t) -> p m t", t=PACK), in_=z_rows[q, g][:].rearrange("p t m -> p m t"))
+            nc.scalar.copy(
+                out=z[:].rearrange("p (c i t) -> p c t i", i=RUN, t=PACK),
+                in_=z_rows[q, g][:].rearrange("p t (c i) -> p c t i", i=RUN),
+            )
 
         def quantise(q, g):
             words = keep.tile([P, QUARTER], U32, name="z_words%d%d" % (q, g), align_bytes=64)
@@ -175,7 +187,7 @@ def tile_ofdm_clipped_transmit_s4_kernel(
         to_quantise = vector_units[-1:] + scalar_units
         groups = [(m0, n0, BANK) for m0 in range(0, SYMBOLS, P) for n0 in range(0, OUTPUTS, BANK)]
         last_m0, last_n0, width = groups.pop()
-        groups.extend([(last_m0, last_n0, width // 2), (last_m0, last_n0 + width // 2, width // 2)])
+        groups.extend([(last_m0, last_n0, width // 2), (last_m0, last_n0 + width // 2, width // 4), (last_m0, last_n0 + 3 * width // 4, width // 4)])
         for j, (m0, n0, width) in enumerate(groups):
             q, m_cols, n_cols = m0 // QUARTER, slice(m0 % QUARTER, m0 % QUARTER + P), slice(n0, n0 + width)
             bank = psum.tile([P, BANK], F32, name="bank")

from contextlib import ExitStack

import concourse.mybir as mybir

SYMBOLS, CARRIERS, SAMPLES, OUTPUTS = 1024, 1024, 2048, 1024
FLOPS = 2 * SYMBOLS * CARRIERS * SAMPLES + 2 * SYMBOLS * SAMPLES * OUTPUTS

F32 = mybir.dt.float32
BF16 = mybir.dt.bfloat16
I32 = mybir.dt.int32
U32 = mybir.dt.uint32
U8 = mybir.dt.uint8
FP4X4 = mybir.dt.float4_e2m1fn_x4
FP8X4 = mybir.dt.float8_e4m3fn_x4
ACT = mybir.ActivationFunctionType
ALU = mybir.AluOpType

P = 128
PACK = 4
K_PASS = P * PACK
PASSES_1 = CARRIERS // K_PASS
PASSES_2 = SAMPLES // K_PASS
QUARTER = 256
QUARTERS = SYMBOLS // QUARTER
BANK = 512
SCALAR_UNITS = 4
RUN = 4
WARM_PASSES = 3


def tile_ofdm_clipped_transmit_s4_kernel(
    tc, sym_words, sym_scales, idft_words, idft_scales, window, fir_words, fir_scales, leak, out
):
    nc = tc.nc
    with ExitStack() as ctx:
        keep = ctx.enter_context(tc.tile_pool(name="keep", bufs=1))
        work = ctx.enter_context(tc.tile_pool(name="work", bufs=4))
        psum = ctx.enter_context(tc.psum_pool(name="psum", bufs=8))
        ctx.enter_context(tc.manual_schedule())

        b_raw = [keep.tile([P, PASSES_1, 2 * K_PASS], U8, name="b_raw%d" % g, align_bytes=64) for g in range(PASSES_2)]
        b_raw_scale = [keep.tile([P, PASSES_1, SAMPLES // 2], U8, name="b_raw_scale%d" % h, align_bytes=64) for h in range(2)]
        x_words = [keep.tile([P, PASSES_1, SYMBOLS], U8, name="x_words%d" % h, align_bytes=64) for h in range(2)]
        x_scale = [keep.tile([P, PASSES_1, SYMBOLS // 2], U8, name="x_scale%d" % h, align_bytes=64) for h in range(2)]
        h_words = [keep.tile([P, OUTPUTS], U32, name="h_words%d" % g, align_bytes=64) for g in range(PASSES_2)]
        h_scale = keep.tile([P, OUTPUTS], U8, align_bytes=64)
        window_bf = keep.tile([P, PASSES_2, PACK], BF16)
        window_f32 = keep.tile([P, PASSES_2, 1, PACK, 1], F32)
        leak_rows = keep.tile([P, OUTPUTS], BF16)

        def flat(t):
            return t[:].rearrange("p g n -> p (g n)").bitcast(I32)

        for h in range(2):
            nc.vector.memset(flat(b_raw_scale[h]), 0)
            nc.vector.memset(flat(x_scale[h]), 0)
        nc.vector.memset(h_scale[:].bitcast(I32), 0)

        def load_b(g):
            cols = slice(g * 2 * K_PASS, (g + 1) * 2 * K_PASS)
            nc.sync.dma_start(out=b_raw[g][:].bitcast(I32), in_=idft_words[:, :, cols].rearrange("g p n -> p g n").bitcast(I32))

        def load_x(h, queue):
            cols = slice(h * SYMBOLS, (h + 1) * SYMBOLS)
            queue.dma_start(out=x_words[h][:].bitcast(I32), in_=sym_words[:, :, cols].rearrange("g p n -> p g n").bitcast(I32))

        def load_scale_rows(planes, scales, h, q, queue):
            width = planes[h].shape[2]
            queue.dma_start(
                out=planes[h][32 * q : 32 * q + 4, :, :].bitcast(I32),
                in_=scales[:, 4 * q : 4 * q + 4, h * width : (h + 1) * width].rearrange("g r n -> r g n").bitcast(I32),
            )

        load_b(0)
        load_x(0, nc.scalar)
        for q in range(4):
            load_scale_rows(b_raw_scale, idft_scales, 0, q, nc.sync)
        for q in range(4):
            load_scale_rows(x_scale, sym_scales, 0, q, nc.scalar if q < 2 else nc.sync)
        load_b(1)
        load_b(2)
        for q in range(4):
            load_scale_rows(b_raw_scale, idft_scales, 1, q, nc.sync)
        load_b(3)
        nc.sync.dma_start(out=window_bf[:], in_=window.rearrange("(g p t) -> p g t", g=PASSES_2, t=PACK))
        load_x(1, nc.sync)
        for q in range(4):
            load_scale_rows(x_scale, sym_scales, 1, q, nc.sync)
        for q in range(4):
            nc.sync.dma_start(out=h_scale[32 * q : 32 * q + 16, :].bitcast(I32), in_=fir_scales[:, 4 * q : 4 * q + 4, :].bitcast(I32))
        for g in range(PASSES_2):
            nc.sync.dma_start(out=h_words[g][:].bitcast(I32), in_=fir_words[g].rearrange("p n t -> p (n t)").bitcast(I32))
        nc.sync.dma_start(out=leak_rows[:], in_=leak.partition_broadcast(P))

        b_words, b_scale = {}, {}
        for g in range(PASSES_2):
            for u in range(2):
                words = keep.tile([P, PASSES_1, 2, P, 2], U8, name="b_words%d%d" % (g, u), align_bytes=64)
                scale = keep.tile([P, PASSES_1, 2, P], U8, name="b_scale%d%d" % (g, u), align_bytes=64)
                src = b_raw[g][:].rearrange("p c (m t b) -> p c t m b", t=PACK, b=2)
                nc.vector.tensor_copy(out=words[:], in_=src[:, :, 2 * u : 2 * u + 2, :, :])
                src = b_raw_scale[g // 2][:, :, g % 2 * K_PASS : (g % 2 + 1) * K_PASS].rearrange("p c (m t) -> p c t m", t=PACK)
                nc.vector.tensor_copy(out=scale[:], in_=src[:, :, 2 * u : 2 * u + 2, :])
                b_words[g, u], b_scale[g, u] = words, scale
        nc.vector.tensor_copy(out=window_f32[:].rearrange("p g o t i -> p g (o t i)"), in_=window_bf[:])

        units = [(q, g) for q in range(QUARTERS) for g in range(PASSES_2)]
        first_half = [(q, g) for g in range(PASSES_2) for q in range(2)]
        vector_units, scalar_units = first_half + units[len(first_half) : -SCALAR_UNITS], units[-SCALAR_UNITS:]
        for i in range(WARM_PASSES):
            bank = psum.tile([P, BANK], F32, name="bank")
            nc.tensor.matmul_mx(
                out=bank[:],
                lhsT=b_raw[0][:, 0, : 2 * P].bitcast(FP4X4),
                lhsT_scale=b_raw_scale[0][:, 0, :P],
                rhs=b_raw[0][:, 0, :].bitcast(FP4X4),
                rhs_scale=b_raw_scale[0][:, 0, :BANK],
                start=True,
                stop=True,
            )

        clipped = {}
        for h in range(2):
            for g in range(PASSES_2):
                clip = keep.tile([P, PACK, BANK], F32, name="clip%d%d" % (h, g))
                clipped[h, g] = clip
                for t in range(PACK):
                    bank = psum.tile([P, BANK], F32, name="bank")
                    for c in range(PASSES_1):
                        nc.tensor.matmul_mx(
                            out=bank[:],
                            lhsT=b_words[g, t // 2][:, c, t % 2, :, :].rearrange("p m b -> p (m b)").bitcast(FP4X4),
                            lhsT_scale=b_scale[g, t // 2][:, c, t % 2, :],
                            rhs=x_words[h][:, c, :].bitcast(FP4X4),
                            rhs_scale=x_scale[h][:, c, :],
                            start=(c == 0),
                            stop=(c == PASSES_1 - 1),
                        )
                    nc.scalar.activation(out=clip[:, t, :], in_=bank[:], func=ACT.Tanh)

        def clip_of(q, g):
            return clipped[q // 2, g][:, :, q % 2 * QUARTER : (q % 2 + 1) * QUARTER]

        z_rows, shaped, z_words, z_scale = {}, {}, {}, {}

        def shape_on_vector(q, g):
            z = work.tile([P, QUARTER * PACK], BF16, name="z_vector", align_bytes=64)
            shaped[q, g] = z
            nc.vector.tensor_tensor(
                out=z[:].rearrange("p (c i t) -> p c t i", i=RUN, t=PACK),
                in0=clip_of(q, g).rearrange("p t (c i) -> p c t i", i=RUN),
                in1=window_f32[:, g, :, :, :].to_broadcast([P, QUARTER // RUN, PACK, RUN]),
                op=ALU.mult,
            )

        def scale_on_scalar(q, g):
            rows = work.tile([P, PACK, QUARTER], BF16, name="z_rows")
            z_rows[q, g] = rows
            src = clip_of(q, g)
            for t in range(PACK):
                nc.scalar.activation(out=rows[:, t, :], in_=src[:, t, :], func=ACT.Copy, scale=window_f32[:, g, 0, t, :])

        def interleave_on_scalar(q, g):
            z = keep.tile([P, QUARTER * PACK], BF16, name="z_scalar%d%d" % (q, g), align_bytes=64)
            shaped[q, g] = z
            nc.scalar.copy(
                out=z[:].rearrange("p (c i t) -> p c t i", i=RUN, t=PACK),
                in_=z_rows[q, g][:].rearrange("p t (c i) -> p c t i", i=RUN),
            )

        def quantise(q, g):
            words = keep.tile([P, QUARTER], U32, name="z_words%d%d" % (q, g), align_bytes=64)
            scale = keep.tile([P, QUARTER], U8, name="z_scale%d%d" % (q, g), align_bytes=64)
            nc.vector.quantize_mx(out=words[:].bitcast(FP8X4), scales=scale[:], in_=shaped[q, g][:])
            z_words[q, g], z_scale[q, g] = words, scale

        for i, unit in enumerate(vector_units):
            shape_on_vector(*unit)
            if i > 0:
                quantise(*vector_units[i - 1])
        for i, unit in enumerate(scalar_units):
            scale_on_scalar(*unit)
            if i > 0:
                interleave_on_scalar(*scalar_units[i - 1])
        interleave_on_scalar(*scalar_units[-1])

        to_quantise = vector_units[-1:] + scalar_units
        groups = [(m0, n0, BANK) for m0 in range(0, SYMBOLS, P) for n0 in range(0, OUTPUTS, BANK)]
        last_m0, last_n0, width = groups.pop()
        groups.extend([(last_m0, last_n0, width // 2), (last_m0, last_n0 + width // 2, width // 4), (last_m0, last_n0 + 3 * width // 4, width // 4)])
        for j, (m0, n0, width) in enumerate(groups):
            q, m_cols, n_cols = m0 // QUARTER, slice(m0 % QUARTER, m0 % QUARTER + P), slice(n0, n0 + width)
            bank = psum.tile([P, BANK], F32, name="bank")
            for g in range(PASSES_2):
                nc.tensor.matmul_mx(
                    out=bank[:, :width],
                    lhsT=z_words[q, g][:, m_cols].bitcast(FP8X4),
                    lhsT_scale=z_scale[q, g][:, m_cols],
                    rhs=h_words[g][:, n_cols].bitcast(FP8X4),
                    rhs_scale=h_scale[4 * g :, n_cols],
                    start=(g == 0),
                    stop=(g == PASSES_2 - 1),
                )
            result = work.tile([P, BANK], F32, name="result", bufs=8)
            nc.vector.tensor_tensor(out=result[:, :width], in0=bank[:, :width], in1=leak_rows[:, n_cols], op=ALU.add)
            nc.sync.dma_start(out=out[m0 : m0 + P, n_cols], in_=result[:, :width])
            if j % 2 == 0 and j // 2 < len(to_quantise):
                quantise(*to_quantise[j // 2])
